import numpy as np
CORES = [77,85,205,213]
N = 4
def setup_inputs(rng):
    return {"x": rng.standard_normal((N, 128, 128), dtype=np.float32)}
def reference(x):
    g = np.ascontiguousarray(x.transpose(1, 2, 0)).reshape(128, 128 * N)
    return {"y": np.broadcast_to(g, (N,) + g.shape)}

@@ -1,0 +1,48 @@
+N = 4
+W = 128
+
+SCRATCH = {
+    "xs": ("sbuf", [128, W], "float32"),
+    "land": ("sbuf", [128, N * W], "float32"),
+}
+SEMAPHORES = ["loaded", "sent", "relay", "arrived", "stored"]
+
+
+def rank_program(g, core, T, topo):
+    cores = list(T.cores)
+    rank = T.rank_of(core)
+    relays = {c + 1: c for c in cores}
+    if rank is None:
+        if core not in relays:
+            return
+        src = relays[core]
+        r = T.rank_of(src)
+        g.wait_ge(T.sem.relay, 16)
+        n = 0
+        for d in cores:
+            if topo.chip(d) % 2 != topo.chip(core) % 2:
+                rid, pid = topo.addr(d, core)
+                g.remote_dma(T.land[:, r * W:(r + 1) * W], T.xs[:], T.sem.arrived, T.sem.sent, pid, rid, 0xFF)
+                n += 8
+        g.wait_ge(T.sem.sent, n)
+        return
+
+    def place(r, src, c0):
+        for p in (0, 64):
+            g.dma_start(T.y[p:p + 64, r::N], src[p:p + 64, c0:c0 + W],
+                        allow_slow_non_contiguous=True).then_inc(T.sem.stored, 16)
+
+    g.dma_start(T.xs[:], T.x[:]).then_inc(T.sem.loaded, 16)
+    g.wait_ge(T.sem.loaded, 16)
+    rid, pid = topo.addr(core + 1, core)
+    g.remote_dma(T.xs[:], T.xs[:], T.sem.relay, T.sem.sent, pid, rid, 0xFFFF)
+    peer = [d for d in cores if d != core and topo.chip(d) % 2 == topo.chip(core) % 2][0]
+    rid, pid = topo.addr(peer, core)
+    g.remote_dma(T.land[:, rank * W:(rank + 1) * W], T.xs[:], T.sem.arrived, T.sem.sent, pid, rid, 0xFF)
+    place(rank, T.xs, 0)
+    g.wait_ge(T.sem.arrived, 24)
+    for r in range(N):
+        if r != rank:
+            place(r, T.land, r * W)
+    g.wait_ge(T.sem.stored, 128)
+    g.wait_ge(T.sem.sent, 24)

@@ -1,48 +1,96 @@
+from concourse.bass import DstId, RemoteDMATransfer
+
 N = 4
-W = 128
+PORT = (2, 3, 6, 7)
+PAIRS = (((0, 9), (0, 10)), ((1, 9), (1, 10)))
+H = 2 * len(PAIRS) * len(PORT)
+NC = 128 // H
 
 SCRATCH = {
-    "xs": ("sbuf", [128, W], "float32"),
-    "land": ("sbuf", [128, N * W], "float32"),
+    "xs": ("dram", [H, 128, NC], "float32"),
+    "pin": ("dram", [N, 128, NC], "float32"),
+    "fwd": ("dram", [2, 128, NC], "float32"),
+    "gp": ("dram", [128, N * NC], "float32"),
+    "gf": ("dram", [H, 128, N * NC], "float32"),
 }
-SEMAPHORES = ["loaded", "sent", "relay", "arrived", "stored"]
+SEMAPHORES = ["loc", "sent", "fin", "pins", "pinx", "garr"]
+
+
+def world(hc, k):
+    return hc[0] * 128 + hc[1] * 8 + k
+
+
+def helper_table():
+    tab = {}
+    k = 0
+    for odd, even in PAIRS:
+        for s in PORT:
+            a, b = world(odd, s), world(even, s)
+            tab[a] = (2 * k, b)
+            tab[b] = (2 * k + 1, a)
+            k += 1
+    return tab
+
+
+def dst(topo, d, core):
+    rid, pid = topo.addr(d, core)
+    return DstId(rid=rid, pnc=pid)
 
 
 def rank_program(g, core, T, topo):
     cores = list(T.cores)
     rank = T.rank_of(core)
-    relays = {c + 1: c for c in cores}
-    if rank is None:
-        if core not in relays:
-            return
-        src = relays[core]
-        r = T.rank_of(src)
-        g.wait_ge(T.sem.relay, 16)
-        n = 0
-        for d in cores:
-            if topo.chip(d) % 2 != topo.chip(core) % 2:
-                rid, pid = topo.addr(d, core)
-                g.remote_dma(T.land[:, r * W:(r + 1) * W], T.xs[:], T.sem.arrived, T.sem.sent, pid, rid, 0xFF)
-                n += 8
-        g.wait_ge(T.sem.sent, n)
+    tab = helper_table()
+    par = topo.chip(core) % 2
+
+    if rank is not None:
+        g.dma_start(T.xs[:], T.x[:]).then_inc(T.sem.loc, 16)
+        g.wait_ge(T.sem.loc, 16)
+        on, off = [], []
+        for what in ("fwd", "pin"):
+            for a, (h, b) in tab.items():
+                if topo.chip(a) % 2 != par:
+                    continue
+                if what == "fwd":
+                    item = (a, T.xs[tab[b][0]], T.fwd[rank // 2], T.sem.fin)
+                else:
+                    item = (a, T.xs[h], T.pin[rank], T.sem.pins)
+                same = (topo.host(a), topo.chip(a)) == (topo.host(core), topo.chip(core))
+                (on if same else off).append(item)
+        nsent = 0
+        while on or off:
+            trs = []
+            engines = list(range(16))
+            for lst, lim in ((off, 8), (on, 16)):
+                while lst and engines and engines[0] < lim:
+                    a, s, d, sem = lst.pop(0)
+                    trs.append(RemoteDMATransfer(dst_ids=[dst(topo, a, core)], dma_engine_mask=1 << engines.pop(0),
+                                                 remote_sem=sem, src=s, dst=d))
+            g.remote_dma_fused(trs, local_sem=T.sem.sent)
+            nsent += len(trs)
+        g.wait_ge(T.sem.garr, 8 * H)
+        g.dma_start(T.y[:], T.gf[:]).then_inc(T.sem.loc, 16)
+        g.wait_ge(T.sem.loc, 32)
+        g.wait_ge(T.sem.sent, nsent)
         return
 
-    def place(r, src, c0):
-        for p in (0, 64):
-            g.dma_start(T.y[p:p + 64, r::N], src[p:p + 64, c0:c0 + W],
-                        allow_slow_non_contiguous=True).then_inc(T.sem.stored, 16)
-
-    g.dma_start(T.xs[:], T.x[:]).then_inc(T.sem.loaded, 16)
-    g.wait_ge(T.sem.loaded, 16)
-    rid, pid = topo.addr(core + 1, core)
-    g.remote_dma(T.xs[:], T.xs[:], T.sem.relay, T.sem.sent, pid, rid, 0xFFFF)
-    peer = [d for d in cores if d != core and topo.chip(d) % 2 == topo.chip(core) % 2][0]
-    rid, pid = topo.addr(peer, core)
-    g.remote_dma(T.land[:, rank * W:(rank + 1) * W], T.xs[:], T.sem.arrived, T.sem.sent, pid, rid, 0xFF)
-    place(rank, T.xs, 0)
-    g.wait_ge(T.sem.arrived, 24)
-    for r in range(N):
-        if r != rank:
-            place(r, T.land, r * W)
-    g.wait_ge(T.sem.stored, 128)
-    g.wait_ge(T.sem.sent, 24)
+    if core not in tab:
+        return
+    h, partner = tab[core]
+    mine = [r for r in range(N) if topo.chip(cores[r]) % 2 == par]
+    other = [r for r in range(N) if r not in mine]
+    g.wait_ge(T.sem.fin, 2)
+    g.remote_dma_fused([RemoteDMATransfer(dst_ids=[dst(topo, partner, core)], dma_engine_mask=0xF << (4 * i),
+                                          remote_sem=T.sem.pinx, src=T.fwd[r // 2], dst=T.pin[r])
+                        for i, r in enumerate(mine)], local_sem=T.sem.sent)
+    g.wait_ge(T.sem.pins, 2)
+    for r in mine:
+        g.dma_start(T.gp[:, r::N], T.pin[r], allow_slow_non_contiguous=True).then_inc(T.sem.loc, 16)
+    g.wait_ge(T.sem.pinx, 8)
+    for r in other:
+        g.dma_start(T.gp[:, r::N], T.pin[r], allow_slow_non_contiguous=True).then_inc(T.sem.loc, 16)
+    g.wait_ge(T.sem.loc, 64)
+    g.remote_dma_fused([RemoteDMATransfer(dst_ids=[dst(topo, d, core) for d in cores], dma_engine_mask=0xFF,
+                                          remote_sem=T.sem.garr, srcs=[T.gp[:]], dsts=[T.gf[h] for d in cores])],
+                       local_sem=T.sem.sent)
+    g.wait_ge(T.sem.sent, 16)

@@ -2,7 +2,7 @@ from concourse.bass import DstId, RemoteDMATransfer
 
 N = 4
 PORT = (2, 3, 6, 7)
-PAIRS = (((0, 9), (0, 10)), ((1, 9), (1, 10)))
+PAIRS = (((0, 9), (0, 8)), ((0, 11), (0, 10)), ((1, 9), (1, 8)), ((1, 11), (1, 10)))
 H = 2 * len(PAIRS) * len(PORT)
 NC = 128 // H
 
@@ -90,7 +90,12 @@ def rank_program(g, core, T, topo):
     for r in other:
         g.dma_start(T.gp[:, r::N], T.pin[r], allow_slow_non_contiguous=True).then_inc(T.sem.loc, 16)
     g.wait_ge(T.sem.loc, 64)
-    g.remote_dma_fused([RemoteDMATransfer(dst_ids=[dst(topo, d, core) for d in cores], dma_engine_mask=0xFF,
-                                          remote_sem=T.sem.garr, srcs=[T.gp[:]], dsts=[T.gf[h] for d in cores])],
-                       local_sem=T.sem.sent)
-    g.wait_ge(T.sem.sent, 16)
+    near = [d for d in cores if (topo.host(d), topo.chip(d)) == (topo.host(core), topo.chip(core))]
+    far = [d for d in cores if d not in near]
+    trs = [RemoteDMATransfer(dst_ids=[dst(topo, d, core) for d in far], dma_engine_mask=0xFF,
+                             remote_sem=T.sem.garr, srcs=[T.gp[:]], dsts=[T.gf[h] for d in far])]
+    if near:
+        trs.append(RemoteDMATransfer(dst_ids=[dst(topo, d, core) for d in near], dma_engine_mask=0xFF00,
+                                     remote_sem=T.sem.garr, srcs=[T.gp[:]], dsts=[T.gf[h] for d in near]))
+    g.remote_dma_fused(trs, local_sem=T.sem.sent)
+    g.wait_ge(T.sem.sent, 8 + 8 * len(trs))

@@ -2,14 +2,15 @@ from concourse.bass import DstId, RemoteDMATransfer
 
 N = 4
 PORT = (2, 3, 6, 7)
-PAIRS = (((0, 9), (0, 8)), ((0, 11), (0, 10)), ((1, 9), (1, 8)), ((1, 11), (1, 10)))
-H = 2 * len(PAIRS) * len(PORT)
+CHIPS = ((0, 8), (0, 9), (0, 10), (0, 11), (1, 8), (1, 9), (1, 10), (1, 11))
+H = len(CHIPS) * len(PORT)
 NC = 128 // H
+NF = len(CHIPS) // 2
 
 SCRATCH = {
     "xs": ("dram", [H, 128, NC], "float32"),
     "pin": ("dram", [N, 128, NC], "float32"),
-    "fwd": ("dram", [2, 128, NC], "float32"),
+    "fwd": ("dram", [NF, 128, NC], "float32"),
     "gp": ("dram", [128, N * NC], "float32"),
     "gf": ("dram", [H, 128, N * NC], "float32"),
 }
@@ -21,15 +22,7 @@ def world(hc, k):
 
 
 def helper_table():
-    tab = {}
-    k = 0
-    for odd, even in PAIRS:
-        for s in PORT:
-            a, b = world(odd, s), world(even, s)
-            tab[a] = (2 * k, b)
-            tab[b] = (2 * k + 1, a)
-            k += 1
-    return tab
+    return {world(hc, s): i * len(PORT) + j for i, hc in enumerate(CHIPS) for j, s in enumerate(PORT)}
 
 
 def dst(topo, d, core):
@@ -37,35 +30,39 @@ def dst(topo, d, core):
     return DstId(rid=rid, pnc=pid)
 
 
+def same_chip(topo, a, b):
+    return (topo.host(a), topo.chip(a)) == (topo.host(b), topo.chip(b))
+
+
 def rank_program(g, core, T, topo):
     cores = list(T.cores)
     rank = T.rank_of(core)
     tab = helper_table()
     par = topo.chip(core) % 2
+    across = [hc for hc in CHIPS if hc[1] % 2 != par]
 
     if rank is not None:
         g.dma_start(T.xs[:], T.x[:]).then_inc(T.sem.loc, 16)
         g.wait_ge(T.sem.loc, 16)
-        on, off = [], []
-        for what in ("fwd", "pin"):
-            for a, (h, b) in tab.items():
-                if topo.chip(a) % 2 != par:
-                    continue
-                if what == "fwd":
-                    item = (a, T.xs[tab[b][0]], T.fwd[rank // 2], T.sem.fin)
-                else:
-                    item = (a, T.xs[h], T.pin[rank], T.sem.pins)
-                same = (topo.host(a), topo.chip(a)) == (topo.host(core), topo.chip(core))
-                (on if same else off).append(item)
-        nsent = 0
+        base = core - core % 8
+        trs = []
+        for s in PORT:
+            for i, hc in enumerate(across):
+                trs.append(RemoteDMATransfer(dst_ids=[dst(topo, base + s, core)], dma_engine_mask=1 << len(trs),
+                                             remote_sem=T.sem.fin, src=T.xs[tab[world(hc, s)]], dst=T.fwd[i]))
+        g.remote_dma_fused(trs, local_sem=T.sem.sent)
+        nsent = len(trs)
+        own = [a for a in tab if topo.chip(a) % 2 == par]
+        on = [a for a in own if same_chip(topo, a, core)]
+        off = [a for a in own if not same_chip(topo, a, core)]
         while on or off:
             trs = []
             engines = list(range(16))
             for lst, lim in ((off, 8), (on, 16)):
                 while lst and engines and engines[0] < lim:
-                    a, s, d, sem = lst.pop(0)
+                    a = lst.pop(0)
                     trs.append(RemoteDMATransfer(dst_ids=[dst(topo, a, core)], dma_engine_mask=1 << engines.pop(0),
-                                                 remote_sem=sem, src=s, dst=d))
+                                                 remote_sem=T.sem.pins, src=T.xs[tab[a]], dst=T.pin[rank]))
             g.remote_dma_fused(trs, local_sem=T.sem.sent)
             nsent += len(trs)
         g.wait_ge(T.sem.garr, 8 * H)
@@ -76,26 +73,30 @@ def rank_program(g, core, T, topo):
 
     if core not in tab:
         return
-    h, partner = tab[core]
+    h = tab[core]
+    nsent = 0
+    near = [d for d in cores if same_chip(topo, d, core)]
+    far = [d for d in cores if d not in near]
+    if near:
+        r = T.rank_of(near[0])
+        g.wait_ge(T.sem.fin, NF)
+        g.remote_dma_fused([RemoteDMATransfer(dst_ids=[dst(topo, world(hc, core % 8), core)], dma_engine_mask=3 << (2 * i),
+                                              remote_sem=T.sem.pinx, src=T.fwd[i], dst=T.pin[r])
+                            for i, hc in enumerate(across)], local_sem=T.sem.sent)
+        nsent += 2 * NF
     mine = [r for r in range(N) if topo.chip(cores[r]) % 2 == par]
     other = [r for r in range(N) if r not in mine]
-    g.wait_ge(T.sem.fin, 2)
-    g.remote_dma_fused([RemoteDMATransfer(dst_ids=[dst(topo, partner, core)], dma_engine_mask=0xF << (4 * i),
-                                          remote_sem=T.sem.pinx, src=T.fwd[r // 2], dst=T.pin[r])
-                        for i, r in enumerate(mine)], local_sem=T.sem.sent)
     g.wait_ge(T.sem.pins, 2)
     for r in mine:
         g.dma_start(T.gp[:, r::N], T.pin[r], allow_slow_non_contiguous=True).then_inc(T.sem.loc, 16)
-    g.wait_ge(T.sem.pinx, 8)
+    g.wait_ge(T.sem.pinx, 4)
     for r in other:
         g.dma_start(T.gp[:, r::N], T.pin[r], allow_slow_non_contiguous=True).then_inc(T.sem.loc, 16)
     g.wait_ge(T.sem.loc, 64)
-    near = [d for d in cores if (topo.host(d), topo.chip(d)) == (topo.host(core), topo.chip(core))]
-    far = [d for d in cores if d not in near]
     trs = [RemoteDMATransfer(dst_ids=[dst(topo, d, core) for d in far], dma_engine_mask=0xFF,
                              remote_sem=T.sem.garr, srcs=[T.gp[:]], dsts=[T.gf[h] for d in far])]
     if near:
         trs.append(RemoteDMATransfer(dst_ids=[dst(topo, d, core) for d in near], dma_engine_mask=0xFF00,
                                      remote_sem=T.sem.garr, srcs=[T.gp[:]], dsts=[T.gf[h] for d in near]))
     g.remote_dma_fused(trs, local_sem=T.sem.sent)
-    g.wait_ge(T.sem.sent, 8 + 8 * len(trs))
+    g.wait_ge(T.sem.sent, nsent + 8 * len(trs))

@@ -1,16 +1,17 @@
 from concourse.bass import DstId, RemoteDMATransfer
 
 N = 4
-PORT = (2, 3, 6, 7)
+DUOS = ((2, 3), (6, 7))
 CHIPS = ((0, 8), (0, 9), (0, 10), (0, 11), (1, 8), (1, 9), (1, 10), (1, 11))
-H = len(CHIPS) * len(PORT)
-NC = 128 // H
-NF = len(CHIPS) // 2
+NBLK = len(CHIPS) * 2
+H = 2 * NBLK
+NB = 128 // NBLK
+NC = NB // 2
 
 SCRATCH = {
-    "xs": ("dram", [H, 128, NC], "float32"),
-    "pin": ("dram", [N, 128, NC], "float32"),
-    "fwd": ("dram", [NF, 128, NC], "float32"),
+    "xs": ("dram", [NBLK, 128, NB], "float32"),
+    "pin": ("dram", [N, 128, NB], "float32"),
+    "fwd": ("dram", [2, 128, NB], "float32"),
     "gp": ("dram", [128, N * NC], "float32"),
     "gf": ("dram", [H, 128, N * NC], "float32"),
 }
@@ -21,8 +22,8 @@ def world(hc, k):
     return hc[0] * 128 + hc[1] * 8 + k
 
 
-def helper_table():
-    return {world(hc, s): i * len(PORT) + j for i, hc in enumerate(CHIPS) for j, s in enumerate(PORT)}
+def block(hc, duo):
+    return CHIPS.index(hc) * 2 + duo
 
 
 def dst(topo, d, core):
@@ -37,61 +38,56 @@ def same_chip(topo, a, b):
 def rank_program(g, core, T, topo):
     cores = list(T.cores)
     rank = T.rank_of(core)
-    tab = helper_table()
     par = topo.chip(core) % 2
+    here = (topo.host(core), topo.chip(core))
     across = [hc for hc in CHIPS if hc[1] % 2 != par]
+    along = [hc for hc in CHIPS if hc[1] % 2 == par]
 
     if rank is not None:
         g.dma_start(T.xs[:], T.x[:]).then_inc(T.sem.loc, 16)
         g.wait_ge(T.sem.loc, 16)
-        base = core - core % 8
-        trs = []
-        for s in PORT:
+        items = []
+        for duo, pc in enumerate(DUOS):
             for i, hc in enumerate(across):
-                trs.append(RemoteDMATransfer(dst_ids=[dst(topo, base + s, core)], dma_engine_mask=1 << len(trs),
-                                             remote_sem=T.sem.fin, src=T.xs[tab[world(hc, s)]], dst=T.fwd[i]))
-        g.remote_dma_fused(trs, local_sem=T.sem.sent)
-        nsent = len(trs)
-        own = [a for a in tab if topo.chip(a) % 2 == par]
-        on = [a for a in own if same_chip(topo, a, core)]
-        off = [a for a in own if not same_chip(topo, a, core)]
-        while on or off:
-            trs = []
-            engines = list(range(16))
-            for lst, lim in ((off, 8), (on, 16)):
-                while lst and engines and engines[0] < lim:
-                    a = lst.pop(0)
-                    trs.append(RemoteDMATransfer(dst_ids=[dst(topo, a, core)], dma_engine_mask=1 << engines.pop(0),
-                                                 remote_sem=T.sem.pins, src=T.xs[tab[a]], dst=T.pin[rank]))
-            g.remote_dma_fused(trs, local_sem=T.sem.sent)
-            nsent += len(trs)
+                items.append((False, [world(here, pc[i // 2])], T.xs[block(hc, duo)], T.fwd[i % 2], T.sem.fin))
+            for hc in along:
+                items.append((hc != here, [world(hc, k) for k in pc], T.xs[block(hc, duo)], T.pin[rank], T.sem.pins))
+        items.sort(key=lambda it: not it[0])
+        g.remote_dma_fused([RemoteDMATransfer(dst_ids=[dst(topo, d, core) for d in ds], dma_engine_mask=1 << e,
+                                              remote_sem=sem, srcs=[s], dsts=[o for d in ds])
+                            for e, (away, ds, s, o, sem) in enumerate(items)], local_sem=T.sem.sent)
         g.wait_ge(T.sem.garr, 8 * H)
         g.dma_start(T.y[:], T.gf[:]).then_inc(T.sem.loc, 16)
         g.wait_ge(T.sem.loc, 32)
-        g.wait_ge(T.sem.sent, nsent)
+        g.wait_ge(T.sem.sent, len(items))
         return
 
-    if core not in tab:
+    k = core % 8
+    if here not in CHIPS or k not in (2, 3, 6, 7):
         return
-    h = tab[core]
+    duo, half = (0, k - 2) if k < 4 else (1, k - 6)
+    h = 2 * block(here, duo) + half
     nsent = 0
     near = [d for d in cores if same_chip(topo, d, core)]
     far = [d for d in cores if d not in near]
     if near:
         r = T.rank_of(near[0])
-        g.wait_ge(T.sem.fin, NF)
-        g.remote_dma_fused([RemoteDMATransfer(dst_ids=[dst(topo, world(hc, core % 8), core)], dma_engine_mask=3 << (2 * i),
-                                              remote_sem=T.sem.pinx, src=T.fwd[i], dst=T.pin[r])
-                            for i, hc in enumerate(across)], local_sem=T.sem.sent)
-        nsent += 2 * NF
+        g.wait_ge(T.sem.fin, 2)
+        g.remote_dma_fused([RemoteDMATransfer(dst_ids=[dst(topo, world(across[2 * half + i], q), core) for q in DUOS[duo]],
+                                              dma_engine_mask=0xF << (4 * i), remote_sem=T.sem.pinx,
+                                              srcs=[T.fwd[i]], dsts=[T.pin[r] for q in DUOS[duo]])
+                            for i in range(2)], local_sem=T.sem.sent)
+        nsent += 8
     mine = [r for r in range(N) if topo.chip(cores[r]) % 2 == par]
     other = [r for r in range(N) if r not in mine]
     g.wait_ge(T.sem.pins, 2)
     for r in mine:
-        g.dma_start(T.gp[:, r::N], T.pin[r], allow_slow_non_contiguous=True).then_inc(T.sem.loc, 16)
-    g.wait_ge(T.sem.pinx, 4)
+        g.dma_start(T.gp[:, r::N], T.pin[r, 64 * half:64 * half + 64, :],
+                    allow_slow_non_contiguous=True).then_inc(T.sem.loc, 16)
+    g.wait_ge(T.sem.pinx, 8)
     for r in other:
-        g.dma_start(T.gp[:, r::N], T.pin[r], allow_slow_non_contiguous=True).then_inc(T.sem.loc, 16)
+        g.dma_start(T.gp[:, r::N], T.pin[r, 64 * half:64 * half + 64, :],
+                    allow_slow_non_contiguous=True).then_inc(T.sem.loc, 16)
     g.wait_ge(T.sem.loc, 64)
     trs = [RemoteDMATransfer(dst_ids=[dst(topo, d, core) for d in far], dma_engine_mask=0xFF,
                              remote_sem=T.sem.garr, srcs=[T.gp[:]], dsts=[T.gf[h] for d in far])]

@@ -1,12 +1,15 @@
 from concourse.bass import DstId, RemoteDMATransfer
 
 N = 4
-DUOS = ((2, 3), (6, 7))
-CHIPS = ((0, 8), (0, 9), (0, 10), (0, 11), (1, 8), (1, 9), (1, 10), (1, 11))
-NBLK = len(CHIPS) * 2
-H = 2 * NBLK
+PORT = (2, 3, 6, 7)
+GROUPS = ((2, 3), (6, 7))
+CHIPS = tuple((hst, c) for hst in (0, 1) for c in range(8, 12))
+GS = len(GROUPS[0])
+NBLK = len(CHIPS) * len(GROUPS)
+H = GS * NBLK
 NB = 128 // NBLK
-NC = NB // 2
+NC = NB // GS
+PR = 128 // GS
 
 SCRATCH = {
     "xs": ("dram", [NBLK, 128, NB], "float32"),
@@ -22,8 +25,8 @@ def world(hc, k):
     return hc[0] * 128 + hc[1] * 8 + k
 
 
-def block(hc, duo):
-    return CHIPS.index(hc) * 2 + duo
+def block(hc, grp):
+    return CHIPS.index(hc) * len(GROUPS) + grp
 
 
 def dst(topo, d, core):
@@ -40,18 +43,17 @@ def rank_program(g, core, T, topo):
     rank = T.rank_of(core)
     par = topo.chip(core) % 2
     here = (topo.host(core), topo.chip(core))
-    across = [hc for hc in CHIPS if hc[1] % 2 != par]
-    along = [hc for hc in CHIPS if hc[1] % 2 == par]
+    across = [(hc, grp) for grp in range(len(GROUPS)) for hc in CHIPS if hc[1] % 2 != par]
+    along = [(hc, grp) for grp in range(len(GROUPS)) for hc in CHIPS if hc[1] % 2 == par]
 
     if rank is not None:
         g.dma_start(T.xs[:], T.x[:]).then_inc(T.sem.loc, 16)
         g.wait_ge(T.sem.loc, 16)
         items = []
-        for duo, pc in enumerate(DUOS):
-            for i, hc in enumerate(across):
-                items.append((False, [world(here, pc[i // 2])], T.xs[block(hc, duo)], T.fwd[i % 2], T.sem.fin))
-            for hc in along:
-                items.append((hc != here, [world(hc, k) for k in pc], T.xs[block(hc, duo)], T.pin[rank], T.sem.pins))
+        for i, (hc, grp) in enumerate(across):
+            items.append((False, [world(here, PORT[i // 2])], T.xs[block(hc, grp)], T.fwd[i % 2], T.sem.fin))
+        for hc, grp in along:
+            items.append((hc != here, [world(hc, k) for k in GROUPS[grp]], T.xs[block(hc, grp)], T.pin[rank], T.sem.pins))
         items.sort(key=lambda it: not it[0])
         g.remote_dma_fused([RemoteDMATransfer(dst_ids=[dst(topo, d, core) for d in ds], dma_engine_mask=1 << e,
                                               remote_sem=sem, srcs=[s], dsts=[o for d in ds])
@@ -63,30 +65,35 @@ def rank_program(g, core, T, topo):
         return
 
     k = core % 8
-    if here not in CHIPS or k not in (2, 3, 6, 7):
+    if here not in CHIPS or k not in PORT:
         return
-    duo, half = (0, k - 2) if k < 4 else (1, k - 6)
-    h = 2 * block(here, duo) + half
+    grp = [k in grp for grp in GROUPS].index(True)
+    part = GROUPS[grp].index(k)
+    h = GS * block(here, grp) + part
     nsent = 0
     near = [d for d in cores if same_chip(topo, d, core)]
     far = [d for d in cores if d not in near]
     if near:
         r = T.rank_of(near[0])
+        j = PORT.index(k)
         g.wait_ge(T.sem.fin, 2)
-        g.remote_dma_fused([RemoteDMATransfer(dst_ids=[dst(topo, world(across[2 * half + i], q), core) for q in DUOS[duo]],
-                                              dma_engine_mask=0xF << (4 * i), remote_sem=T.sem.pinx,
-                                              srcs=[T.fwd[i]], dsts=[T.pin[r] for q in DUOS[duo]])
-                            for i in range(2)], local_sem=T.sem.sent)
+        trs = []
+        for i in range(2):
+            hc, gq = across[2 * j + i]
+            trs.append(RemoteDMATransfer(dst_ids=[dst(topo, world(hc, q), core) for q in GROUPS[gq]],
+                                         dma_engine_mask=0xF << (4 * i), remote_sem=T.sem.pinx,
+                                         srcs=[T.fwd[i]], dsts=[T.pin[r] for q in GROUPS[gq]]))
+        g.remote_dma_fused(trs, local_sem=T.sem.sent)
         nsent += 8
     mine = [r for r in range(N) if topo.chip(cores[r]) % 2 == par]
     other = [r for r in range(N) if r not in mine]
     g.wait_ge(T.sem.pins, 2)
     for r in mine:
-        g.dma_start(T.gp[:, r::N], T.pin[r, 64 * half:64 * half + 64, :],
+        g.dma_start(T.gp[:, r::N], T.pin[r, PR * part:PR * part + PR, :],
                     allow_slow_non_contiguous=True).then_inc(T.sem.loc, 16)
     g.wait_ge(T.sem.pinx, 8)
     for r in other:
-        g.dma_start(T.gp[:, r::N], T.pin[r, 64 * half:64 * half + 64, :],
+        g.dma_start(T.gp[:, r::N], T.pin[r, PR * part:PR * part + PR, :],
                     allow_slow_non_contiguous=True).then_inc(T.sem.loc, 16)
     g.wait_ge(T.sem.loc, 64)
     trs = [RemoteDMATransfer(dst_ids=[dst(topo, d, core) for d in far], dma_engine_mask=0xFF,

from concourse.bass import DstId, RemoteDMATransfer

N = 4
PORT = (2, 3, 6, 7)
GROUPS = ((2, 3), (6, 7))
CHIPS = tuple((hst, c) for hst in (0, 1) for c in range(8, 12))
GS = len(GROUPS[0])
NBLK = len(CHIPS) * len(GROUPS)
H = GS * NBLK
NB = 128 // NBLK
NC = NB // GS
PR = 128 // GS

SCRATCH = {
    "xs": ("dram", [NBLK, 128, NB], "float32"),
    "pin": ("dram", [N, 128, NB], "float32"),
    "fwd": ("dram", [2, 128, NB], "float32"),
    "gp": ("dram", [128, N * NC], "float32"),
    "gf": ("dram", [H, 128, N * NC], "float32"),
}
SEMAPHORES = ["loc", "sent", "fin", "pins", "pinx", "garr"]


def world(hc, k):
    return hc[0] * 128 + hc[1] * 8 + k


def block(hc, grp):
    return CHIPS.index(hc) * len(GROUPS) + grp


def dst(topo, d, core):
    rid, pid = topo.addr(d, core)
    return DstId(rid=rid, pnc=pid)


def same_chip(topo, a, b):
    return (topo.host(a), topo.chip(a)) == (topo.host(b), topo.chip(b))


def rank_program(g, core, T, topo):
    cores = list(T.cores)
    rank = T.rank_of(core)
    par = topo.chip(core) % 2
    here = (topo.host(core), topo.chip(core))
    across = [(hc, grp) for grp in range(len(GROUPS)) for hc in CHIPS if hc[1] % 2 != par]
    along = [(hc, grp) for grp in range(len(GROUPS)) for hc in CHIPS if hc[1] % 2 == par]

    if rank is not None:
        g.dma_start(T.xs[:], T.x[:]).then_inc(T.sem.loc, 16)
        g.wait_ge(T.sem.loc, 16)
        items = []
        for i, (hc, grp) in enumerate(across):
            items.append((False, [world(here, PORT[i // 2])], T.xs[block(hc, grp)], T.fwd[i % 2], T.sem.fin))
        for hc, grp in along:
            items.append((hc != here, [world(hc, k) for k in GROUPS[grp]], T.xs[block(hc, grp)], T.pin[rank], T.sem.pins))
        items.sort(key=lambda it: not it[0])
        g.remote_dma_fused([RemoteDMATransfer(dst_ids=[dst(topo, d, core) for d in ds], dma_engine_mask=1 << e,
                                              remote_sem=sem, srcs=[s], dsts=[o for d in ds])
                            for e, (away, ds, s, o, sem) in enumerate(items)], local_sem=T.sem.sent)
        g.wait_ge(T.sem.garr, 8 * H)
        g.dma_start(T.y[:], T.gf[:]).then_inc(T.sem.loc, 16)
        g.wait_ge(T.sem.loc, 32)
        g.wait_ge(T.sem.sent, len(items))
        return

    k = core % 8
    if here not in CHIPS or k not in PORT:
        return
    grp = [k in grp for grp in GROUPS].index(True)
    part = GROUPS[grp].index(k)
    h = GS * block(here, grp) + part
    nsent = 0
    near = [d for d in cores if same_chip(topo, d, core)]
    far = [d for d in cores if d not in near]
    if near:
        r = T.rank_of(near[0])
        j = PORT.index(k)
        g.wait_ge(T.sem.fin, 2)
        trs = []
        for i in range(2):
            hc, gq = across[2 * j + i]
            trs.append(RemoteDMATransfer(dst_ids=[dst(topo, world(hc, q), core) for q in GROUPS[gq]],
                                         dma_engine_mask=0xF << (4 * i), remote_sem=T.sem.pinx,
                                         srcs=[T.fwd[i]], dsts=[T.pin[r] for q in GROUPS[gq]]))
        g.remote_dma_fused(trs, local_sem=T.sem.sent)
        nsent += 8
    mine = [r for r in range(N) if topo.chip(cores[r]) % 2 == par]
    other = [r for r in range(N) if r not in mine]
    g.wait_ge(T.sem.pins, 2)
    for r in mine:
        g.dma_start(T.gp[:, r::N], T.pin[r, PR * part:PR * part + PR, :],
                    allow_slow_non_contiguous=True).then_inc(T.sem.loc, 16)
    g.wait_ge(T.sem.pinx, 8)
    for r in other:
        g.dma_start(T.gp[:, r::N], T.pin[r, PR * part:PR * part + PR, :],
                    allow_slow_non_contiguous=True).then_inc(T.sem.loc, 16)
    g.wait_ge(T.sem.loc, 64)
    trs = [RemoteDMATransfer(dst_ids=[dst(topo, d, core) for d in far], dma_engine_mask=0xFF,
                             remote_sem=T.sem.garr, srcs=[T.gp[:]], dsts=[T.gf[h] for d in far])]
    if near:
        trs.append(RemoteDMATransfer(dst_ids=[dst(topo, d, core) for d in near], dma_engine_mask=0xFF00,
                                     remote_sem=T.sem.garr, srcs=[T.gp[:]], dsts=[T.gf[h] for d in near]))
    g.remote_dma_fused(trs, local_sem=T.sem.sent)
    g.wait_ge(T.sem.sent, nsent + 8 * len(trs))
